import numpy as np
CORES = [2,130,10,138,18,146,26,154,34,162,42,170,50,178,58,186]
N = 16
T = 512
ROUTE = [[[12],[12],[12],[13],[5],[9],[12],[12],[12],[7],[14],[13],[1],[12],[12],[12],[5],[15],[6],[13],[14],[12],[15],[12],[9],[15],[10],[12],[12],[2],[3],[0],[8],[6],[7],[7],[3],[15],[8],[15],[6],[8],[12],[12],[12],[4],[12],[3],[5],[14],[12],[12],[3],[12],[12],[12],[12],[12],[12],[12],[14],[1],[7],[1],[0],[14],[5],[12],[12],[12],[12],[12],[12],[9],[3],[5],[12],[12],[5],[11],[12],[1],[0],[12],[3],[12],[12],[12],[12],[3],[10],[7],[12],[12],[12],[9],[10],[5],[15],[12],[12],[6],[12],[9],[0],[13],[12],[12],[12],[7],[12],[1],[12],[12],[12],[1],[12],[0],[12],[9],[7],[12],[6],[12],[9],[3],[4],[0],[12],[0],[12],[12],[15],[11],[12],[12],[12],[12],[12],[2],[1],[0],[12],[7],[9],[0],[10],[1],[7],[2],[12],[12],[3],[5],[12],[10],[11],[12],[12],[11],[15],[8],[12],[12],[4],[7],[12],[12],[11],[10],[0],[8],[12],[2],[12],[6],[15],[6],[12],[12],[12],[2],[12],[14],[8],[12],[5],[8],[12],[11],[12],[8],[13],[13],[12],[1],[12],[14],[12],[10],[12],[14],[12],[5],[12],[15],[13],[7],[12],[12],[12],[3],[6],[12],[4],[15],[9],[12],[2],[9],[12],[12],[0],[12],[12],[12],[12],[12],[12],[15],[12],[4],[12],[12],[12],[10],[10],[4],[3],[1],[1],[14],[12],[12],[12],[9],[12],[12],[13],[11],[12],[0],[12],[12],[13],[12],[2],[12],[10],[2],[15],[12],[12],[6],[12],[8],[12],[9],[1],[15],[12],[15],[7],[8],[1],[12],[12],[12],[0],[11],[12],[12],[10],[3],[9],[11],[12],[12],[12],[8],[5],[12],[12],[12],[7],[12],[12],[7],[12],[15],[12],[7],[1],[5],[8],[12],[8],[2],[12],[12],[14],[1],[10],[12],[5],[12],[12],[12],[12],[11],[8],[9],[12],[4],[12],[12],[6],[12],[12],[11],[12],[12],[12],[12],[15],[12],[12],[15],[15],[15],[10],[3],[9],[12],[8],[13],[12],[12],[1],[12],[0],[8],[12],[12],[12],[9],[9],[11],[6],[12],[13],[9],[12],[12],[10],[12],[12],[5],[11],[12],[12],[5],[12],[12],[12],[5],[15],[12],[12],[0],[0],[12],[12],[12],[12],[5],[8],[12],[12],[7],[6],[6],[12],[12],[9],[0],[12],[12],[5],[12],[9],[12],[12],[12],[11],[15],[12],[4],[12],[5],[12],[10],[9],[12],[0],[1],[13],[12],[12],[12],[12],[3],[2],[2],[12],[12],[2],[12],[12],[12],[2],[11],[15],[1],[4],[11],[1],[12],[12],[9],[10],[3],[14],[12],[7],[13],[7],[8],[12],[12],[12],[2],[10],[12],[14],[12],[12],[7],[12],[12],[11],[11],[15],[1],[12],[12],[7],[12],[15],[13],[1],[12],[12],[9],[12],[1],[12],[8],[11],[12],[6],[12],[12],[2],[14],[12],[13],[12],[12],[8],[6],[12],[12],[5],[12],[13],[5],[12],[4],[8],[4],[12],[12],[12],[2],[13],[12],[12],[12],[12],[7],[11]],[[9],[7],[12],[12],[0],[12],[12],[13],[12],[12],[9],[12],[12],[8],[14],[12],[12],[15],[12],[12],[11],[12],[11],[3],[12],[12],[9],[13],[10],[12],[12],[12],[5],[12],[2],[12],[12],[12],[15],[12],[12],[14],[12],[2],[12],[6],[6],[12],[14],[12],[12],[11],[14],[9],[12],[12],[14],[12],[12],[12],[0],[12],[4],[7],[8],[2],[5],[4],[12],[0],[0],[12],[12],[2],[4],[12],[12],[10],[14],[12],[15],[9],[12],[0],[1],[13],[12],[5],[12],[12],[2],[5],[12],[12],[12],[12],[15],[15],[6],[12],[1],[2],[5],[12],[10],[15],[9],[13],[12],[10],[15],[12],[3],[12],[4],[12],[14],[3],[12],[3],[15],[12],[12],[12],[12],[12],[12],[12],[12],[12],[9],[1],[12],[12],[1],[12],[12],[12],[4],[12],[12],[14],[12],[12],[7],[2],[13],[0],[12],[1],[9],[9],[8],[7],[12],[12],[12],[2],[3],[9],[12],[10],[3],[15],[6],[9],[12],[15],[12],[12],[12],[11],[5],[13],[14],[12],[12],[12],[12],[12],[15],[12],[15],[8],[7],[9],[12],[12],[12],[9],[10],[12],[15],[11],[14],[12],[12],[7],[14],[12],[7],[2],[12],[13],[8],[12],[0],[12],[0],[9],[12],[3],[12],[11],[12],[15],[12],[12],[3],[2],[3],[4],[12],[12],[12],[12],[3],[12],[9],[4],[9],[12],[8],[2],[12],[11],[15],[12],[12],[12],[4],[12],[12],[2],[14],[12],[10],[13],[7],[0],[3],[3],[12],[1],[0],[8],[12],[5],[12],[7],[12],[15],[12],[10],[12],[10],[0],[7],[12],[14],[12],[1],[12],[3],[12],[3],[12],[12],[0],[13],[15],[12],[8],[9],[6],[12],[5],[5],[0],[12],[15],[13],[12],[12],[12],[10],[12],[12],[6],[12],[5],[12],[13],[12],[1],[1],[12],[12],[11],[12],[12],[12],[13],[12],[13],[12],[12],[1],[12],[12],[11],[8],[4],[12],[6],[12],[12],[8],[0],[12],[12],[11],[6],[7],[14],[11],[9],[11],[11],[12],[12],[2],[12],[12],[2],[12],[12],[12],[12],[4],[12],[12],[12],[12],[14],[4],[10],[12],[3],[10],[13],[12],[0],[9],[8],[12],[0],[3],[12],[12],[0],[0],[12],[9],[12],[11],[3],[15],[12],[12],[12],[12],[14],[12],[12],[9],[12],[9],[4],[12],[12],[11],[12],[1],[15],[2],[12],[12],[10],[11],[12],[12],[12],[3],[2],[5],[12],[12],[12],[12],[12],[12],[12],[15],[13],[8],[12],[12],[12],[12],[12],[11],[14],[9],[12],[14],[6],[12],[12],[12],[10],[12],[12],[12],[12],[12],[12],[12],[12],[8],[12],[15],[4],[12],[11],[7],[9],[12],[14],[7],[3],[12],[12],[12],[2],[12],[12],[6],[13],[9],[0],[10],[12],[11],[12],[12],[9],[3],[3],[12],[11],[12],[15],[12],[12],[1],[12],[3],[10],[12],[4],[12],[8],[13],[12],[4],[12],[12],[13],[4],[12],[12],[9],[15],[5],[12],[2],[1],[12],[12],[12],[12],[2],[14],[15],[8],[11],[12],[9],[12],[11],[12]],[[12],[12],[15],[6],[11],[14],[0],[7],[12],[12],[12],[12],[6],[0],[8],[3],[1],[13],[5],[12],[12],[12],[2],[12],[10],[2],[12],[14],[8],[4],[11],[5],[12],[12],[5],[12],[12],[11],[12],[12],[3],[6],[14],[5],[15],[0],[7],[1],[12],[13],[12],[12],[1],[2],[12],[12],[5],[15],[1],[11],[13],[0],[12],[9],[12],[6],[14],[3],[2],[3],[2],[12],[11],[9],[3],[5],[15],[14],[12],[0],[10],[1],[12],[12],[12],[3],[0],[12],[12],[12],[8],[12],[12],[7],[12],[9],[11],[12],[11],[12],[12],[13],[12],[12],[12],[6],[15],[7],[0],[12],[1],[12],[12],[15],[12],[14],[12],[12],[4],[10],[9],[15],[12],[9],[12],[14],[3],[11],[12],[13],[7],[6],[8],[12],[12],[7],[14],[11],[11],[12],[10],[11],[13],[12],[12],[12],[9],[14],[3],[11],[12],[12],[12],[4],[13],[7],[10],[1],[15],[8],[12],[14],[13],[3],[6],[12],[8],[12],[9],[12],[6],[15],[2],[12],[12],[8],[12],[8],[12],[4],[11],[11],[12],[12],[1],[3],[2],[2],[12],[12],[9],[8],[12],[4],[11],[14],[15],[11],[12],[12],[12],[13],[12],[9],[12],[12],[2],[10],[0],[3],[5],[12],[12],[15],[12],[12],[9],[13],[2],[7],[6],[11],[12],[4],[12],[0],[0],[2],[11],[12],[12],[0],[12],[12],[5],[12],[5],[12],[1],[12],[15],[10],[15],[10],[12],[12],[6],[12],[12],[11],[3],[3],[12],[15],[1],[15],[5],[12],[12],[12],[12],[10],[4],[0],[12],[6],[1],[0],[12],[12],[10],[12],[8],[0],[12],[12],[12],[12],[12],[12],[7],[11],[14],[12],[7],[1],[11],[10],[12],[12],[1],[2],[12],[15],[4],[12],[12],[10],[12],[12],[12],[12],[9],[12],[13],[12],[13],[0],[12],[12],[12],[14],[12],[12],[12],[12],[13],[12],[10],[12],[12],[12],[13],[9],[12],[12],[6],[10],[4],[12],[11],[3],[2],[12],[12],[12],[13],[5],[9],[12],[15],[2],[12],[12],[12],[13],[12],[9],[6],[12],[12],[2],[9],[0],[12],[12],[15],[12],[2],[9],[12],[12],[1],[15],[0],[12],[12],[14],[12],[12],[12],[12],[6],[12],[0],[15],[12],[12],[12],[3],[9],[12],[12],[0],[9],[12],[12],[6],[12],[8],[15],[0],[8],[14],[12],[12],[9],[12],[14],[12],[12],[12],[12],[12],[1],[12],[6],[12],[12],[12],[3],[12],[11],[12],[12],[12],[12],[10],[12],[12],[5],[12],[12],[2],[12],[12],[12],[12],[12],[12],[12],[12],[1],[12],[5],[12],[12],[11],[5],[4],[12],[4],[0],[2],[14],[12],[12],[12],[8],[6],[0],[12],[13],[12],[12],[12],[4],[4],[10],[12],[14],[8],[2],[13],[13],[12],[12],[8],[7],[2],[11],[1],[7],[9],[12],[12],[10],[12],[10],[7],[12],[12],[12],[8],[13],[12],[3],[12],[12],[12],[1],[12],[5],[14],[12],[12],[1],[12],[12],[7],[9],[4],[12],[9],[11],[12],[12],[14],[12],[12],[9],[6]],[[12],[12],[12],[4],[12],[1],[12],[12],[15],[12],[12],[8],[4],[12],[12],[8],[13],[12],[5],[8],[12],[9],[12],[12],[4],[12],[12],[11],[12],[12],[0],[13],[7],[12],[12],[14],[12],[12],[4],[12],[12],[13],[12],[14],[12],[12],[12],[12],[12],[4],[12],[3],[12],[12],[12],[0],[12],[13],[4],[2],[12],[12],[12],[12],[12],[12],[14],[12],[5],[12],[12],[12],[12],[14],[11],[15],[13],[2],[5],[12],[11],[9],[12],[11],[9],[7],[9],[2],[12],[11],[7],[12],[2],[8],[2],[12],[14],[12],[12],[12],[12],[8],[12],[12],[12],[11],[10],[4],[1],[12],[12],[11],[12],[9],[12],[12],[1],[2],[12],[2],[15],[12],[7],[6],[8],[12],[7],[12],[14],[10],[7],[12],[13],[1],[8],[11],[14],[7],[3],[0],[12],[15],[1],[12],[10],[12],[12],[10],[14],[14],[1],[2],[12],[12],[11],[12],[12],[7],[14],[4],[12],[12],[13],[10],[12],[7],[12],[9],[14],[11],[3],[11],[0],[3],[12],[12],[10],[15],[4],[12],[12],[1],[13],[5],[12],[12],[1],[4],[3],[13],[12],[12],[8],[15],[12],[2],[12],[12],[12],[11],[10],[14],[5],[10],[12],[12],[12],[10],[12],[1],[15],[10],[12],[12],[12],[12],[12],[10],[12],[12],[8],[12],[1],[13],[12],[7],[12],[12],[12],[6],[12],[12],[12],[0],[12],[5],[3],[12],[12],[10],[1],[12],[12],[12],[7],[7],[1],[9],[8],[14],[12],[12],[12],[9],[6],[15],[3],[13],[12],[13],[12],[12],[10],[12],[12],[8],[12],[12],[12],[6],[12],[5],[15],[0],[12],[12],[8],[12],[8],[10],[9],[8],[4],[3],[12],[13],[2],[13],[9],[13],[1],[7],[12],[12],[12],[14],[12],[12],[12],[10],[1],[4],[12],[10],[3],[11],[11],[8],[9],[2],[12],[12],[15],[15],[8],[8],[10],[14],[11],[12],[8],[13],[2],[12],[4],[11],[12],[12],[15],[6],[2],[12],[11],[12],[12],[2],[12],[12],[0],[12],[12],[1],[4],[12],[12],[12],[12],[12],[2],[11],[1],[11],[1],[13],[12],[12],[12],[12],[12],[7],[4],[12],[3],[14],[0],[0],[13],[12],[14],[12],[8],[5],[14],[4],[12],[11],[2],[12],[12],[7],[11],[5],[12],[11],[5],[13],[3],[12],[3],[6],[9],[5],[12],[12],[12],[12],[12],[12],[8],[12],[12],[8],[12],[1],[12],[12],[12],[13],[12],[11],[14],[12],[12],[11],[12],[1],[12],[12],[3],[12],[12],[8],[11],[12],[10],[7],[12],[9],[12],[12],[7],[12],[15],[1],[2],[12],[2],[12],[12],[12],[15],[2],[12],[12],[6],[12],[12],[12],[5],[11],[12],[8],[9],[12],[4],[12],[12],[6],[12],[15],[12],[12],[12],[4],[3],[12],[12],[12],[2],[1],[12],[7],[12],[12],[15],[12],[11],[13],[12],[12],[7],[4],[12],[12],[1],[12],[13],[12],[12],[8],[12],[13],[5],[3],[12],[5],[12],[14],[4],[12],[12],[12],[8],[5],[12],[7],[11],[12],[12],[12],[4],[8]],[[12],[12],[2],[8],[7],[0],[2],[12],[7],[1],[12],[12],[12],[2],[6],[0],[12],[13],[11],[11],[2],[12],[10],[13],[0],[6],[12],[2],[12],[2],[11],[12],[12],[12],[13],[12],[12],[0],[8],[7],[0],[3],[12],[3],[6],[7],[12],[7],[14],[12],[12],[12],[10],[6],[5],[4],[10],[0],[10],[1],[12],[2],[8],[12],[15],[12],[6],[3],[14],[12],[10],[2],[1],[12],[12],[13],[12],[14],[12],[12],[1],[9],[15],[8],[15],[7],[12],[5],[12],[12],[1],[8],[9],[12],[15],[2],[0],[9],[5],[4],[6],[12],[0],[8],[8],[12],[12],[15],[12],[4],[13],[5],[12],[5],[8],[12],[12],[4],[12],[12],[12],[4],[12],[6],[3],[12],[12],[12],[4],[14],[7],[8],[4],[4],[6],[1],[12],[13],[12],[4],[12],[12],[0],[8],[12],[14],[10],[6],[11],[12],[3],[12],[12],[12],[13],[12],[12],[10],[5],[1],[8],[12],[12],[4],[8],[8],[12],[14],[12],[14],[4],[10],[12],[12],[14],[6],[12],[1],[5],[6],[12],[12],[1],[12],[12],[12],[12],[12],[15],[12],[12],[12],[12],[12],[15],[15],[12],[14],[12],[1],[12],[0],[11],[2],[15],[12],[4],[12],[15],[6],[12],[12],[12],[9],[12],[0],[5],[6],[9],[12],[12],[13],[12],[12],[12],[12],[15],[3],[4],[12],[1],[3],[7],[6],[12],[5],[4],[3],[0],[12],[2],[11],[1],[14],[11],[2],[12],[15],[4],[6],[6],[0],[12],[12],[3],[12],[12],[3],[0],[12],[12],[12],[5],[8],[12],[12],[0],[15],[15],[12],[12],[12],[10],[12],[12],[7],[12],[3],[3],[12],[13],[12],[11],[0],[12],[12],[9],[8],[12],[1],[14],[0],[11],[12],[12],[12],[5],[12],[12],[5],[12],[3],[0],[7],[12],[12],[12],[12],[12],[4],[1],[13],[0],[15],[6],[8],[12],[9],[6],[12],[4],[9],[8],[11],[9],[12],[12],[12],[12],[11],[12],[12],[4],[12],[12],[12],[0],[10],[12],[13],[9],[12],[12],[13],[12],[10],[12],[14],[1],[12],[10],[7],[10],[8],[6],[12],[14],[2],[11],[14],[12],[12],[8],[12],[4],[4],[12],[4],[6],[4],[12],[7],[2],[12],[12],[9],[13],[11],[5],[1],[12],[13],[9],[12],[12],[12],[12],[12],[7],[15],[4],[12],[10],[12],[12],[7],[9],[8],[2],[6],[2],[12],[5],[12],[12],[12],[12],[5],[12],[6],[12],[3],[12],[2],[11],[12],[9],[15],[12],[4],[12],[11],[12],[12],[12],[4],[12],[14],[0],[12],[12],[1],[12],[12],[0],[12],[6],[12],[12],[12],[12],[12],[12],[12],[12],[4],[7],[12],[10],[11],[12],[11],[12],[12],[2],[4],[12],[4],[4],[6],[12],[4],[12],[12],[9],[12],[11],[12],[9],[12],[0],[12],[11],[6],[12],[15],[7],[8],[12],[14],[12],[12],[0],[12],[12],[12],[12],[12],[8],[3],[6],[6],[12],[13],[12],[12],[6],[12],[12],[12],[12],[0],[12],[13],[12],[12],[2],[6],[12],[2],[1],[0]],[[12],[7],[14],[10],[4],[12],[12],[12],[13],[12],[8],[11],[12],[6],[14],[12],[12],[3],[3],[2],[12],[13],[12],[12],[3],[12],[12],[8],[1],[6],[11],[10],[9],[12],[7],[0],[8],[3],[12],[12],[13],[2],[14],[1],[12],[11],[3],[12],[9],[12],[12],[8],[15],[12],[14],[12],[6],[12],[12],[7],[7],[2],[1],[3],[4],[1],[12],[14],[12],[12],[10],[12],[2],[12],[2],[10],[8],[12],[12],[6],[12],[15],[6],[1],[7],[12],[5],[12],[0],[12],[2],[12],[0],[4],[0],[9],[12],[12],[14],[10],[3],[9],[9],[2],[12],[12],[12],[15],[12],[12],[12],[13],[8],[10],[12],[7],[12],[12],[13],[12],[12],[1],[12],[12],[9],[12],[5],[5],[15],[14],[14],[0],[12],[12],[14],[12],[11],[10],[13],[12],[12],[4],[12],[13],[12],[12],[10],[12],[9],[14],[13],[12],[12],[7],[2],[13],[12],[12],[9],[12],[12],[12],[11],[12],[12],[8],[15],[15],[5],[12],[10],[14],[14],[12],[6],[9],[1],[8],[12],[3],[5],[9],[12],[12],[15],[12],[4],[12],[12],[12],[4],[2],[7],[12],[0],[12],[0],[2],[12],[12],[12],[3],[8],[0],[12],[6],[14],[15],[10],[12],[12],[12],[3],[12],[6],[3],[12],[1],[3],[12],[12],[1],[12],[12],[3],[12],[7],[12],[12],[8],[12],[12],[13],[12],[7],[13],[4],[13],[13],[8],[0],[15],[5],[12],[9],[0],[5],[12],[12],[12],[8],[7],[12],[2],[12],[5],[13],[13],[12],[12],[12],[15],[2],[5],[12],[12],[12],[12],[12],[11],[10],[9],[12],[10],[12],[12],[1],[12],[12],[10],[13],[12],[12],[0],[13],[14],[12],[9],[5],[13],[15],[0],[12],[12],[7],[4],[7],[12],[12],[0],[12],[5],[12],[10],[15],[9],[12],[13],[8],[15],[12],[7],[12],[12],[12],[12],[8],[12],[12],[12],[6],[13],[12],[12],[15],[12],[12],[14],[12],[12],[13],[4],[12],[12],[13],[0],[11],[12],[11],[7],[12],[11],[11],[14],[14],[12],[12],[1],[10],[12],[12],[3],[0],[12],[5],[14],[1],[12],[5],[12],[0],[0],[12],[10],[0],[12],[12],[8],[5],[12],[12],[10],[12],[14],[10],[12],[5],[12],[1],[14],[12],[12],[12],[8],[7],[7],[6],[12],[12],[2],[7],[3],[13],[12],[12],[3],[0],[12],[9],[12],[12],[2],[12],[0],[5],[12],[12],[12],[4],[12],[4],[12],[12],[12],[12],[6],[12],[12],[15],[12],[12],[12],[10],[12],[11],[12],[12],[15],[12],[12],[6],[12],[7],[14],[12],[12],[13],[12],[12],[10],[8],[5],[12],[9],[12],[12],[1],[8],[5],[4],[6],[12],[6],[12],[15],[2],[12],[12],[12],[8],[13],[0],[9],[12],[12],[12],[14],[12],[12],[15],[6],[12],[12],[12],[12],[4],[12],[7],[12],[12],[15],[5],[12],[12],[12],[9],[12],[13],[10],[12],[12],[15],[5],[7],[12],[3],[5],[12],[8],[7],[12],[12],[3],[12],[12],[15],[5],[2],[12],[12],[12],[2]],[[2],[1],[12],[13],[12],[11],[12],[12],[12],[3],[4],[12],[12],[2],[12],[5],[12],[8],[0],[1],[2],[12],[12],[4],[5],[13],[14],[14],[12],[4],[12],[12],[10],[0],[12],[12],[5],[12],[8],[8],[4],[10],[8],[14],[13],[12],[12],[12],[15],[12],[2],[9],[12],[12],[10],[12],[2],[0],[14],[13],[2],[8],[5],[9],[12],[4],[12],[12],[1],[5],[12],[14],[12],[12],[0],[2],[12],[4],[0],[12],[4],[12],[13],[12],[2],[4],[13],[11],[13],[8],[11],[5],[5],[6],[12],[11],[1],[13],[13],[12],[12],[12],[7],[14],[14],[12],[12],[15],[11],[11],[9],[12],[1],[8],[9],[15],[5],[12],[12],[12],[9],[14],[12],[12],[5],[12],[9],[6],[12],[12],[12],[12],[12],[12],[12],[8],[12],[12],[6],[12],[4],[6],[3],[12],[13],[2],[2],[12],[12],[12],[15],[12],[12],[15],[6],[12],[12],[12],[12],[0],[3],[1],[12],[12],[11],[10],[12],[12],[14],[12],[5],[10],[8],[15],[10],[12],[12],[12],[12],[12],[12],[12],[1],[12],[2],[1],[12],[12],[0],[3],[9],[12],[12],[6],[0],[9],[6],[8],[12],[12],[14],[12],[14],[12],[12],[8],[12],[12],[0],[12],[8],[10],[12],[12],[12],[12],[12],[4],[0],[12],[14],[12],[6],[3],[12],[5],[2],[12],[10],[4],[10],[3],[1],[15],[12],[5],[14],[14],[9],[12],[7],[12],[12],[12],[12],[12],[9],[15],[12],[12],[12],[12],[8],[12],[6],[13],[12],[12],[5],[12],[5],[9],[0],[0],[12],[12],[5],[8],[2],[12],[5],[12],[13],[4],[12],[12],[7],[12],[2],[1],[12],[7],[4],[2],[12],[12],[12],[12],[12],[7],[11],[2],[6],[12],[13],[4],[12],[12],[5],[12],[3],[12],[10],[12],[7],[12],[12],[9],[12],[12],[12],[11],[4],[12],[0],[9],[12],[12],[8],[7],[12],[6],[7],[12],[14],[12],[9],[15],[3],[9],[3],[13],[8],[12],[9],[12],[11],[12],[12],[3],[12],[0],[4],[13],[11],[11],[0],[12],[15],[12],[12],[12],[5],[7],[12],[14],[12],[11],[14],[0],[0],[12],[10],[12],[2],[0],[9],[14],[7],[2],[12],[9],[12],[12],[8],[13],[12],[1],[12],[14],[5],[1],[11],[12],[12],[12],[12],[12],[5],[9],[3],[8],[6],[8],[3],[12],[12],[12],[12],[4],[5],[9],[12],[12],[7],[15],[12],[12],[12],[5],[12],[7],[1],[8],[3],[4],[12],[0],[12],[12],[9],[14],[2],[6],[5],[6],[5],[0],[12],[12],[10],[12],[12],[4],[9],[12],[12],[12],[12],[12],[0],[3],[7],[12],[12],[7],[14],[12],[12],[12],[3],[12],[12],[2],[12],[4],[12],[12],[0],[2],[9],[12],[12],[7],[12],[12],[12],[12],[4],[11],[12],[12],[11],[5],[1],[12],[10],[12],[12],[3],[12],[12],[9],[7],[12],[12],[10],[4],[3],[12],[12],[12],[5],[12],[7],[11],[10],[12],[8],[12],[12],[12],[3],[12],[1],[13],[14],[12],[11],[12],[12],[12]],[[11],[12],[12],[12],[0],[6],[12],[1],[13],[7],[15],[3],[12],[0],[12],[12],[4],[14],[12],[12],[12],[12],[8],[9],[8],[1],[12],[8],[12],[12],[3],[9],[12],[0],[5],[0],[1],[11],[12],[2],[12],[12],[1],[12],[12],[5],[12],[12],[12],[11],[12],[13],[7],[10],[1],[9],[12],[10],[8],[12],[5],[11],[2],[9],[12],[13],[7],[12],[12],[12],[13],[12],[1],[12],[12],[12],[5],[12],[2],[12],[0],[9],[1],[12],[12],[12],[6],[12],[12],[10],[12],[7],[3],[0],[12],[6],[12],[12],[14],[6],[12],[3],[13],[15],[12],[12],[12],[2],[12],[12],[7],[14],[12],[12],[12],[3],[12],[12],[14],[12],[12],[15],[12],[12],[12],[7],[14],[12],[10],[11],[11],[14],[12],[7],[3],[3],[5],[0],[12],[2],[6],[13],[0],[13],[12],[10],[12],[7],[12],[12],[15],[12],[12],[12],[0],[8],[14],[12],[8],[11],[11],[12],[12],[12],[15],[13],[6],[12],[12],[12],[12],[12],[12],[2],[12],[12],[12],[1],[12],[12],[12],[1],[12],[13],[7],[7],[12],[12],[10],[1],[12],[12],[12],[1],[12],[0],[12],[12],[10],[1],[12],[12],[6],[13],[13],[12],[3],[14],[3],[12],[13],[15],[14],[1],[1],[3],[15],[12],[8],[6],[1],[14],[12],[3],[12],[12],[8],[12],[1],[12],[12],[14],[12],[12],[12],[12],[3],[0],[12],[12],[12],[7],[12],[3],[8],[14],[12],[15],[12],[12],[10],[12],[0],[12],[2],[6],[14],[11],[12],[12],[2],[15],[3],[12],[12],[9],[12],[11],[14],[6],[12],[12],[15],[12],[1],[12],[12],[12],[12],[0],[5],[6],[15],[12],[14],[15],[12],[0],[12],[13],[15],[6],[3],[12],[12],[12],[14],[8],[12],[11],[14],[3],[12],[12],[12],[12],[15],[14],[12],[15],[15],[12],[10],[0],[12],[11],[0],[12],[11],[8],[12],[12],[12],[12],[1],[12],[12],[5],[3],[12],[12],[14],[1],[12],[12],[12],[12],[15],[3],[13],[0],[4],[12],[12],[0],[2],[12],[12],[14],[5],[15],[15],[5],[9],[12],[13],[5],[0],[13],[13],[12],[12],[12],[0],[12],[12],[12],[12],[12],[2],[14],[2],[1],[6],[4],[11],[2],[14],[13],[1],[12],[8],[12],[2],[10],[5],[1],[12],[7],[12],[6],[12],[0],[2],[12],[12],[0],[12],[12],[3],[14],[12],[14],[12],[7],[12],[1],[3],[12],[12],[12],[7],[12],[12],[12],[14],[12],[4],[1],[1],[12],[14],[12],[12],[10],[8],[12],[12],[12],[5],[11],[12],[12],[12],[12],[8],[12],[7],[12],[12],[12],[12],[12],[12],[15],[5],[7],[10],[13],[5],[12],[9],[10],[12],[12],[12],[15],[12],[12],[12],[12],[0],[9],[12],[6],[12],[12],[5],[13],[1],[2],[1],[15],[3],[12],[2],[12],[7],[11],[2],[13],[12],[12],[12],[7],[12],[12],[7],[3],[9],[10],[5],[1],[12],[12],[12],[10],[15],[5],[15],[10],[12],[12],[13],[11],[9],[12],[12],[3],[15],[12],[12]],[[15],[4],[12],[12],[13],[12],[3],[7],[9],[12],[12],[12],[12],[6],[12],[10],[15],[15],[12],[12],[12],[4],[4],[1],[3],[4],[12],[14],[8],[12],[15],[7],[6],[12],[14],[6],[13],[12],[12],[12],[5],[12],[11],[3],[12],[9],[7],[2],[12],[15],[12],[12],[9],[10],[10],[0],[14],[12],[12],[7],[0],[12],[9],[5],[12],[12],[3],[12],[12],[12],[12],[12],[14],[12],[12],[1],[9],[12],[8],[9],[0],[13],[4],[10],[10],[4],[12],[3],[11],[3],[7],[5],[5],[12],[4],[1],[15],[12],[12],[5],[12],[8],[12],[12],[12],[12],[13],[12],[2],[12],[12],[12],[12],[12],[8],[12],[4],[12],[12],[3],[14],[14],[12],[0],[0],[12],[10],[8],[2],[0],[12],[12],[10],[12],[8],[13],[12],[12],[14],[12],[12],[12],[10],[12],[12],[12],[1],[12],[4],[13],[12],[14],[12],[12],[12],[4],[2],[1],[0],[2],[12],[8],[0],[8],[1],[10],[14],[9],[12],[0],[12],[3],[2],[6],[13],[12],[12],[2],[12],[12],[12],[13],[13],[12],[12],[12],[12],[8],[14],[12],[1],[6],[4],[12],[12],[15],[12],[2],[11],[12],[12],[15],[10],[12],[8],[4],[10],[2],[12],[11],[12],[12],[12],[12],[12],[12],[11],[13],[12],[14],[7],[12],[13],[14],[8],[12],[11],[15],[12],[6],[12],[12],[12],[12],[12],[7],[9],[12],[8],[12],[9],[15],[14],[13],[12],[12],[12],[12],[10],[15],[3],[12],[2],[0],[9],[3],[12],[5],[12],[10],[0],[12],[14],[14],[3],[3],[3],[12],[12],[12],[10],[9],[15],[3],[12],[14],[12],[10],[12],[11],[0],[8],[12],[0],[0],[11],[0],[12],[12],[12],[14],[8],[0],[12],[8],[0],[1],[12],[12],[12],[8],[8],[15],[12],[12],[12],[12],[12],[8],[9],[12],[12],[2],[12],[12],[15],[8],[9],[12],[12],[12],[12],[12],[12],[12],[11],[11],[12],[14],[1],[12],[11],[10],[11],[12],[12],[9],[0],[8],[12],[12],[1],[10],[12],[12],[12],[9],[11],[9],[12],[12],[2],[1],[9],[10],[10],[7],[0],[10],[5],[12],[12],[4],[12],[12],[13],[12],[12],[11],[12],[7],[12],[4],[3],[12],[8],[0],[9],[15],[12],[10],[12],[15],[12],[12],[8],[12],[12],[5],[8],[12],[12],[3],[2],[9],[0],[12],[14],[12],[12],[12],[2],[2],[12],[1],[2],[13],[9],[12],[12],[12],[13],[12],[4],[6],[12],[12],[12],[12],[13],[11],[12],[6],[12],[3],[0],[12],[4],[12],[7],[9],[15],[12],[12],[2],[3],[5],[12],[15],[12],[12],[12],[7],[3],[12],[3],[6],[4],[4],[5],[12],[12],[12],[12],[12],[12],[0],[0],[14],[4],[15],[11],[10],[3],[13],[14],[12],[12],[15],[8],[12],[2],[11],[12],[11],[15],[6],[8],[12],[3],[4],[12],[12],[12],[7],[7],[2],[3],[4],[7],[8],[12],[10],[12],[6],[11],[12],[12],[0],[12],[5],[12],[8],[12],[9],[12],[12],[11],[12],[11],[3],[8]],[[12],[11],[0],[7],[14],[0],[12],[12],[9],[8],[12],[2],[12],[12],[15],[12],[10],[12],[15],[8],[12],[9],[1],[3],[9],[12],[2],[1],[14],[11],[12],[12],[11],[0],[12],[7],[14],[0],[12],[12],[12],[9],[13],[8],[7],[7],[12],[13],[12],[4],[12],[12],[7],[8],[12],[7],[12],[12],[12],[10],[12],[1],[8],[12],[12],[5],[13],[12],[1],[12],[2],[12],[12],[12],[8],[3],[12],[12],[10],[0],[12],[12],[9],[8],[12],[12],[10],[9],[12],[14],[12],[12],[0],[12],[12],[3],[3],[3],[12],[7],[15],[8],[12],[12],[12],[15],[12],[12],[2],[12],[12],[0],[12],[13],[12],[12],[6],[12],[12],[2],[12],[12],[12],[12],[10],[6],[6],[13],[12],[12],[12],[12],[12],[8],[5],[0],[12],[12],[1],[12],[4],[3],[12],[6],[10],[12],[10],[4],[12],[11],[12],[12],[4],[14],[11],[0],[12],[13],[11],[12],[12],[12],[13],[12],[8],[2],[13],[5],[7],[9],[12],[12],[0],[12],[12],[0],[12],[10],[3],[9],[15],[9],[2],[0],[12],[12],[12],[0],[6],[15],[13],[2],[12],[12],[12],[12],[12],[2],[12],[12],[12],[12],[13],[9],[5],[12],[12],[12],[3],[12],[4],[12],[12],[14],[12],[9],[12],[3],[15],[12],[9],[9],[6],[12],[12],[12],[8],[12],[8],[13],[12],[11],[12],[2],[12],[10],[11],[12],[1],[12],[1],[2],[0],[12],[14],[12],[1],[13],[1],[13],[3],[12],[12],[12],[9],[13],[8],[12],[12],[10],[8],[12],[7],[9],[13],[2],[12],[12],[7],[12],[12],[3],[10],[15],[8],[12],[9],[12],[3],[3],[12],[12],[12],[12],[1],[12],[12],[12],[12],[12],[1],[11],[12],[12],[11],[12],[5],[12],[5],[7],[5],[12],[12],[12],[9],[1],[15],[12],[7],[12],[15],[12],[12],[12],[14],[12],[12],[12],[14],[1],[7],[12],[12],[0],[5],[12],[12],[13],[12],[13],[3],[11],[5],[12],[12],[12],[11],[12],[12],[4],[12],[12],[2],[1],[4],[15],[4],[8],[0],[12],[6],[12],[12],[12],[12],[8],[1],[11],[1],[11],[4],[12],[0],[15],[15],[2],[12],[11],[8],[12],[13],[8],[2],[7],[12],[12],[12],[8],[12],[7],[4],[4],[12],[5],[9],[12],[13],[2],[4],[15],[12],[12],[1],[12],[12],[12],[12],[0],[12],[7],[4],[12],[12],[13],[12],[12],[13],[12],[9],[5],[12],[13],[15],[12],[12],[12],[3],[2],[12],[12],[14],[8],[3],[3],[12],[15],[15],[10],[12],[12],[12],[15],[12],[12],[12],[12],[5],[4],[4],[7],[13],[12],[1],[12],[3],[13],[3],[12],[10],[12],[12],[2],[14],[1],[1],[15],[12],[10],[6],[12],[6],[1],[12],[7],[15],[7],[1],[12],[12],[0],[12],[9],[14],[6],[12],[0],[9],[1],[1],[10],[12],[5],[12],[15],[3],[12],[7],[12],[12],[15],[12],[12],[12],[7],[10],[12],[3],[12],[12],[6],[12],[12],[8],[12],[6],[12],[0],[9],[6],[12],[3],[0]],[[12],[6],[12],[12],[13],[12],[9],[1],[1],[0],[12],[5],[14],[3],[14],[7],[0],[12],[5],[12],[15],[12],[5],[12],[13],[9],[10],[9],[12],[8],[12],[12],[2],[12],[12],[12],[13],[0],[12],[12],[12],[12],[12],[5],[12],[12],[12],[12],[3],[12],[14],[4],[12],[12],[9],[1],[12],[12],[1],[15],[12],[13],[11],[5],[12],[12],[10],[3],[8],[12],[12],[13],[11],[12],[13],[7],[15],[2],[2],[12],[2],[12],[6],[4],[13],[3],[12],[5],[12],[9],[12],[9],[8],[1],[12],[2],[4],[12],[12],[12],[8],[12],[5],[0],[7],[13],[0],[0],[13],[3],[10],[0],[14],[12],[8],[10],[12],[12],[14],[12],[7],[12],[12],[5],[3],[2],[13],[12],[9],[11],[12],[6],[15],[12],[11],[12],[12],[6],[11],[12],[12],[12],[12],[8],[6],[9],[12],[12],[11],[12],[9],[12],[10],[12],[14],[12],[12],[7],[7],[9],[2],[12],[12],[13],[12],[12],[11],[12],[10],[11],[3],[4],[12],[12],[0],[13],[15],[12],[12],[12],[10],[6],[15],[14],[7],[3],[13],[12],[6],[12],[10],[12],[13],[14],[14],[6],[15],[9],[4],[6],[9],[9],[10],[12],[12],[13],[12],[3],[10],[3],[0],[12],[12],[9],[10],[9],[0],[12],[8],[12],[3],[4],[2],[8],[8],[8],[12],[12],[6],[1],[4],[3],[10],[0],[15],[12],[12],[14],[13],[12],[12],[12],[2],[12],[8],[12],[10],[12],[12],[12],[12],[8],[12],[5],[12],[5],[12],[9],[12],[4],[12],[12],[7],[14],[12],[6],[4],[14],[2],[7],[8],[12],[11],[12],[13],[0],[5],[12],[5],[12],[12],[0],[12],[3],[0],[13],[12],[11],[12],[0],[15],[10],[8],[3],[3],[2],[13],[3],[11],[12],[14],[12],[12],[15],[12],[12],[12],[12],[12],[3],[4],[14],[13],[12],[12],[12],[0],[12],[2],[14],[8],[12],[1],[12],[12],[12],[12],[12],[12],[12],[4],[12],[7],[12],[13],[12],[11],[4],[11],[7],[12],[12],[7],[12],[12],[3],[11],[10],[15],[12],[12],[6],[12],[2],[12],[12],[12],[12],[5],[7],[12],[1],[12],[1],[4],[3],[12],[12],[1],[12],[4],[12],[10],[12],[1],[0],[12],[12],[11],[12],[12],[2],[12],[12],[5],[12],[9],[12],[7],[11],[1],[5],[6],[1],[12],[8],[12],[1],[3],[12],[6],[14],[6],[15],[6],[12],[5],[10],[11],[12],[4],[12],[13],[4],[6],[9],[1],[11],[12],[12],[4],[3],[8],[10],[12],[9],[7],[13],[12],[1],[12],[5],[12],[12],[0],[12],[8],[2],[13],[12],[4],[4],[13],[12],[12],[2],[12],[8],[11],[10],[12],[12],[6],[12],[7],[12],[12],[9],[12],[1],[5],[12],[4],[11],[12],[14],[12],[12],[15],[6],[12],[7],[13],[12],[12],[4],[0],[12],[15],[12],[12],[8],[1],[12],[12],[12],[0],[2],[8],[12],[13],[6],[15],[4],[7],[12],[1],[8],[8],[8],[12],[12],[15],[6],[4],[12],[15],[12],[5],[12],[12],[8]],[[15],[12],[12],[10],[5],[12],[4],[0],[7],[8],[12],[12],[1],[9],[10],[11],[12],[12],[3],[0],[12],[12],[12],[12],[10],[12],[12],[4],[6],[13],[6],[4],[14],[5],[0],[12],[7],[12],[12],[11],[8],[12],[12],[10],[7],[12],[12],[2],[1],[12],[12],[13],[4],[12],[12],[8],[12],[12],[12],[4],[12],[9],[14],[10],[13],[6],[12],[12],[3],[12],[12],[14],[14],[12],[6],[13],[0],[7],[12],[12],[12],[9],[12],[3],[12],[10],[12],[12],[12],[7],[3],[12],[5],[3],[11],[8],[12],[12],[12],[12],[3],[4],[2],[1],[9],[12],[12],[2],[12],[11],[13],[10],[12],[14],[12],[5],[10],[2],[14],[10],[12],[7],[12],[12],[8],[7],[9],[12],[12],[12],[12],[12],[12],[12],[3],[2],[2],[12],[7],[8],[3],[14],[9],[7],[5],[12],[12],[4],[3],[2],[0],[14],[1],[13],[12],[14],[9],[12],[10],[0],[12],[5],[10],[12],[12],[12],[2],[12],[12],[4],[5],[6],[12],[3],[8],[12],[10],[1],[12],[13],[2],[13],[12],[12],[12],[15],[0],[2],[12],[14],[12],[8],[12],[12],[0],[3],[12],[2],[5],[2],[12],[12],[12],[3],[6],[12],[14],[12],[14],[7],[5],[12],[7],[2],[8],[2],[12],[12],[12],[14],[6],[1],[8],[15],[15],[9],[14],[12],[9],[12],[12],[12],[5],[6],[12],[12],[5],[8],[15],[4],[6],[12],[12],[14],[12],[15],[8],[3],[11],[12],[12],[1],[12],[12],[12],[0],[12],[8],[1],[12],[14],[3],[12],[6],[11],[15],[3],[8],[14],[12],[7],[7],[2],[15],[12],[12],[1],[12],[4],[14],[12],[6],[12],[7],[12],[3],[11],[12],[12],[12],[4],[9],[12],[12],[12],[12],[7],[12],[12],[12],[12],[3],[12],[12],[10],[6],[8],[12],[12],[12],[12],[12],[3],[12],[3],[12],[8],[14],[12],[12],[12],[8],[12],[12],[7],[6],[12],[12],[12],[11],[14],[12],[12],[4],[7],[5],[4],[11],[8],[2],[12],[5],[12],[0],[12],[12],[0],[12],[13],[12],[5],[8],[6],[9],[7],[13],[12],[9],[12],[12],[13],[12],[0],[12],[6],[3],[13],[12],[8],[4],[12],[12],[6],[2],[9],[12],[1],[12],[10],[2],[12],[12],[4],[14],[12],[7],[12],[12],[12],[7],[7],[12],[6],[12],[12],[12],[6],[12],[9],[12],[12],[12],[12],[9],[7],[12],[15],[12],[12],[12],[9],[12],[12],[12],[12],[12],[12],[12],[12],[0],[12],[1],[6],[8],[12],[4],[15],[8],[12],[12],[12],[3],[5],[12],[12],[11],[6],[4],[12],[10],[10],[12],[2],[2],[4],[2],[14],[10],[12],[9],[0],[2],[12],[3],[14],[12],[4],[10],[2],[2],[12],[1],[12],[12],[12],[1],[12],[12],[12],[12],[0],[3],[3],[12],[3],[12],[2],[13],[6],[12],[6],[8],[15],[2],[12],[12],[2],[0],[12],[12],[12],[12],[3],[10],[0],[12],[1],[0],[12],[15],[4],[12],[12],[12],[6],[13],[12],[12],[4],[11],[7],[10]],[[12],[6],[12],[5],[12],[8],[14],[0],[2],[3],[2],[8],[12],[9],[6],[12],[15],[12],[15],[4],[9],[12],[12],[12],[11],[12],[2],[11],[5],[7],[3],[6],[2],[6],[12],[12],[1],[11],[9],[9],[13],[12],[12],[4],[13],[5],[12],[1],[10],[12],[12],[9],[9],[12],[14],[6],[14],[12],[12],[12],[15],[12],[7],[13],[13],[12],[0],[1],[12],[12],[6],[15],[10],[7],[2],[12],[1],[7],[8],[12],[12],[12],[4],[12],[12],[14],[0],[12],[13],[8],[12],[6],[1],[15],[12],[12],[12],[12],[12],[12],[12],[12],[2],[12],[1],[12],[9],[3],[7],[12],[12],[11],[12],[12],[12],[9],[12],[12],[12],[12],[14],[2],[3],[12],[5],[12],[12],[2],[13],[3],[6],[15],[14],[0],[12],[3],[8],[1],[3],[5],[12],[12],[12],[12],[12],[10],[2],[9],[12],[7],[12],[12],[5],[14],[8],[12],[12],[12],[12],[12],[14],[2],[12],[14],[12],[4],[12],[1],[12],[0],[5],[12],[12],[14],[6],[13],[12],[12],[2],[0],[12],[7],[5],[12],[12],[12],[12],[14],[4],[12],[7],[13],[12],[4],[12],[14],[12],[12],[3],[8],[15],[1],[12],[12],[10],[12],[12],[0],[2],[12],[3],[1],[0],[8],[3],[0],[12],[2],[12],[12],[12],[9],[5],[15],[12],[12],[12],[11],[14],[13],[4],[14],[12],[13],[12],[12],[12],[14],[12],[12],[7],[9],[5],[7],[9],[13],[12],[12],[7],[12],[4],[12],[8],[12],[12],[4],[12],[10],[2],[0],[12],[13],[7],[12],[0],[12],[9],[12],[2],[6],[4],[12],[13],[12],[14],[1],[15],[11],[14],[12],[12],[12],[12],[10],[12],[0],[12],[7],[2],[12],[15],[5],[8],[0],[12],[12],[12],[12],[5],[12],[8],[12],[12],[8],[12],[12],[12],[12],[12],[8],[12],[8],[11],[15],[12],[12],[4],[12],[12],[15],[12],[15],[3],[15],[12],[12],[3],[9],[1],[14],[13],[13],[1],[12],[9],[12],[12],[12],[3],[12],[12],[14],[12],[12],[12],[12],[0],[12],[7],[12],[12],[9],[2],[2],[5],[12],[12],[15],[12],[12],[14],[10],[10],[9],[11],[7],[11],[7],[12],[3],[5],[5],[13],[0],[7],[7],[3],[12],[12],[13],[5],[13],[12],[12],[12],[15],[7],[12],[7],[12],[3],[8],[6],[12],[12],[1],[2],[14],[12],[12],[4],[3],[11],[6],[7],[12],[12],[6],[0],[6],[14],[13],[12],[11],[9],[12],[8],[15],[12],[15],[4],[1],[13],[0],[4],[12],[5],[12],[12],[10],[9],[4],[12],[1],[12],[2],[12],[12],[12],[7],[13],[9],[8],[12],[3],[12],[4],[1],[13],[13],[12],[0],[3],[12],[11],[12],[12],[12],[12],[4],[0],[12],[14],[12],[12],[8],[12],[7],[12],[12],[3],[1],[12],[12],[0],[12],[7],[12],[4],[10],[12],[12],[12],[12],[14],[12],[12],[12],[14],[8],[12],[12],[4],[4],[3],[7],[9],[9],[6],[12],[4],[14],[14],[1],[5],[12],[12],[14],[9],[12],[12],[12]],[[3],[11],[15],[13],[12],[9],[3],[1],[4],[12],[6],[12],[4],[12],[4],[12],[12],[0],[2],[12],[12],[12],[12],[0],[0],[2],[0],[12],[12],[12],[12],[1],[15],[5],[7],[4],[12],[12],[9],[1],[9],[2],[12],[12],[11],[12],[5],[1],[12],[1],[9],[12],[12],[10],[5],[9],[8],[4],[12],[6],[12],[12],[12],[3],[12],[12],[12],[7],[13],[12],[4],[12],[12],[11],[9],[0],[5],[5],[7],[0],[12],[9],[11],[12],[12],[10],[12],[0],[12],[3],[12],[11],[12],[8],[12],[12],[12],[12],[12],[9],[15],[12],[15],[1],[12],[0],[11],[12],[2],[12],[12],[12],[12],[12],[12],[12],[12],[1],[12],[12],[12],[1],[12],[10],[12],[12],[15],[12],[14],[13],[12],[2],[12],[3],[6],[12],[12],[1],[4],[12],[12],[11],[0],[12],[12],[14],[10],[12],[12],[15],[14],[7],[11],[12],[10],[11],[12],[12],[7],[4],[14],[7],[3],[9],[12],[12],[6],[12],[10],[15],[12],[12],[12],[12],[12],[10],[1],[13],[1],[11],[11],[3],[12],[12],[7],[12],[12],[15],[12],[12],[12],[8],[12],[1],[12],[13],[0],[12],[12],[12],[2],[15],[5],[6],[12],[11],[12],[2],[8],[12],[4],[12],[12],[12],[12],[12],[2],[7],[15],[12],[12],[12],[12],[10],[1],[12],[6],[3],[12],[7],[12],[12],[12],[12],[7],[13],[12],[3],[13],[6],[7],[12],[4],[13],[6],[1],[14],[12],[2],[12],[12],[7],[4],[0],[8],[3],[2],[12],[12],[11],[12],[4],[12],[12],[2],[14],[0],[2],[5],[11],[3],[12],[12],[15],[12],[5],[12],[12],[12],[0],[12],[1],[7],[12],[14],[12],[12],[12],[12],[0],[12],[12],[3],[11],[13],[15],[4],[12],[12],[12],[12],[12],[15],[2],[12],[9],[12],[12],[9],[0],[12],[5],[12],[3],[11],[15],[4],[12],[1],[7],[10],[12],[9],[12],[12],[4],[2],[12],[8],[9],[13],[4],[14],[6],[13],[12],[12],[6],[5],[1],[15],[12],[12],[12],[12],[9],[3],[12],[12],[11],[9],[12],[12],[12],[15],[7],[12],[7],[15],[3],[15],[12],[15],[12],[7],[12],[13],[10],[12],[3],[12],[12],[4],[13],[12],[11],[12],[4],[4],[3],[8],[13],[12],[12],[13],[12],[12],[15],[12],[0],[12],[12],[12],[12],[12],[12],[12],[12],[14],[4],[4],[9],[5],[15],[10],[14],[6],[12],[8],[12],[12],[3],[12],[4],[1],[13],[12],[6],[14],[12],[12],[12],[11],[12],[7],[12],[12],[12],[1],[11],[12],[12],[12],[3],[14],[10],[12],[15],[4],[6],[12],[11],[13],[2],[1],[11],[12],[3],[14],[8],[2],[12],[12],[12],[6],[12],[12],[12],[7],[12],[11],[8],[10],[0],[12],[7],[10],[3],[1],[11],[13],[12],[12],[12],[13],[11],[1],[8],[12],[3],[12],[12],[12],[12],[8],[10],[12],[2],[12],[12],[13],[12],[7],[6],[11],[5],[12],[12],[1],[12],[12],[3],[12],[12],[12],[1],[12],[9],[9],[12],[12],[6]],[[9],[8],[14],[8],[11],[11],[6],[12],[12],[12],[5],[8],[13],[12],[15],[1],[12],[0],[7],[12],[6],[2],[5],[12],[9],[15],[12],[12],[0],[12],[8],[5],[12],[2],[10],[4],[12],[5],[12],[12],[5],[1],[12],[12],[12],[6],[1],[12],[11],[13],[12],[12],[4],[12],[0],[10],[12],[13],[12],[5],[10],[8],[12],[12],[14],[7],[12],[9],[6],[1],[2],[10],[11],[4],[12],[0],[11],[12],[7],[12],[10],[12],[12],[14],[13],[1],[12],[0],[15],[11],[11],[14],[12],[8],[2],[12],[7],[14],[3],[12],[1],[12],[12],[8],[12],[12],[12],[14],[12],[12],[12],[12],[12],[11],[12],[8],[2],[3],[10],[12],[6],[4],[12],[7],[14],[12],[12],[12],[4],[8],[3],[9],[12],[9],[13],[15],[12],[12],[12],[14],[12],[12],[12],[6],[12],[8],[12],[14],[12],[8],[13],[12],[12],[12],[0],[6],[5],[12],[12],[12],[8],[6],[10],[12],[3],[0],[15],[6],[12],[12],[2],[14],[12],[11],[12],[6],[12],[4],[14],[11],[12],[0],[12],[12],[4],[1],[11],[14],[12],[12],[9],[5],[0],[8],[12],[14],[5],[12],[12],[12],[5],[12],[9],[11],[0],[12],[15],[12],[12],[12],[0],[12],[11],[12],[15],[6],[12],[0],[3],[12],[12],[3],[10],[5],[12],[5],[1],[3],[8],[9],[12],[12],[1],[7],[13],[12],[12],[12],[12],[12],[12],[12],[4],[12],[12],[13],[12],[7],[2],[12],[12],[11],[5],[12],[13],[12],[5],[13],[0],[12],[5],[12],[6],[12],[12],[5],[9],[14],[6],[12],[15],[3],[10],[3],[11],[8],[12],[12],[12],[1],[8],[5],[12],[13],[12],[12],[12],[12],[14],[2],[12],[12],[10],[9],[13],[12],[1],[12],[12],[15],[14],[12],[15],[12],[12],[3],[10],[12],[12],[5],[12],[12],[12],[1],[8],[9],[1],[12],[0],[12],[3],[9],[15],[5],[13],[12],[14],[4],[12],[7],[9],[2],[2],[11],[6],[11],[3],[5],[4],[12],[14],[12],[12],[6],[12],[7],[1],[12],[1],[12],[11],[11],[9],[3],[8],[12],[12],[12],[12],[12],[0],[4],[4],[7],[8],[12],[0],[14],[12],[12],[12],[11],[12],[7],[12],[12],[4],[12],[1],[2],[12],[2],[5],[13],[12],[5],[12],[12],[12],[12],[12],[2],[12],[14],[12],[12],[3],[1],[12],[6],[12],[0],[3],[6],[14],[12],[13],[2],[9],[12],[2],[8],[12],[4],[12],[12],[5],[3],[12],[4],[12],[15],[5],[12],[8],[5],[7],[12],[12],[1],[8],[11],[12],[12],[10],[12],[1],[12],[3],[14],[11],[12],[6],[12],[12],[10],[11],[7],[12],[12],[12],[12],[1],[12],[9],[4],[8],[12],[1],[4],[7],[12],[7],[12],[12],[12],[12],[8],[12],[13],[9],[12],[3],[12],[15],[12],[9],[12],[12],[12],[12],[12],[7],[12],[5],[2],[4],[12],[9],[6],[12],[12],[6],[5],[3],[6],[14],[12],[12],[6],[12],[12],[12],[7],[12],[2],[11],[9],[7],[12],[2],[14]],[[12],[12],[12],[12],[6],[7],[9],[12],[9],[12],[3],[12],[9],[12],[15],[11],[15],[8],[9],[12],[12],[12],[1],[12],[8],[12],[14],[12],[5],[0],[12],[12],[15],[10],[3],[13],[12],[12],[12],[2],[12],[12],[12],[12],[2],[12],[12],[2],[12],[14],[8],[12],[14],[1],[0],[5],[11],[4],[15],[12],[2],[12],[1],[12],[13],[12],[12],[12],[12],[12],[12],[2],[3],[14],[5],[12],[12],[10],[12],[1],[12],[10],[12],[12],[12],[12],[12],[13],[9],[10],[14],[14],[15],[7],[10],[9],[12],[12],[8],[7],[12],[14],[12],[14],[9],[0],[0],[0],[0],[12],[12],[3],[11],[12],[4],[12],[12],[12],[12],[12],[6],[1],[9],[14],[12],[12],[12],[4],[6],[12],[12],[12],[8],[10],[15],[10],[12],[8],[3],[7],[10],[5],[5],[1],[12],[9],[12],[12],[12],[13],[2],[1],[10],[1],[11],[12],[13],[0],[13],[3],[3],[13],[15],[11],[5],[3],[12],[12],[12],[12],[7],[12],[11],[12],[3],[12],[12],[12],[12],[8],[12],[7],[10],[7],[15],[0],[10],[12],[14],[13],[4],[12],[12],[12],[7],[1],[12],[12],[4],[12],[5],[12],[6],[12],[0],[12],[3],[1],[12],[11],[12],[1],[9],[12],[3],[6],[12],[6],[9],[8],[1],[7],[7],[0],[6],[12],[10],[3],[9],[2],[12],[12],[2],[12],[4],[12],[12],[5],[10],[12],[2],[15],[1],[12],[12],[11],[12],[8],[2],[0],[7],[3],[12],[12],[12],[0],[12],[12],[12],[8],[12],[12],[11],[12],[11],[2],[5],[15],[4],[12],[13],[5],[14],[4],[10],[12],[6],[12],[4],[12],[5],[2],[14],[5],[0],[8],[13],[2],[10],[12],[11],[12],[3],[12],[7],[14],[11],[12],[12],[12],[15],[5],[1],[12],[11],[12],[3],[12],[12],[12],[2],[12],[12],[12],[6],[14],[6],[1],[12],[12],[12],[8],[0],[15],[14],[5],[6],[12],[0],[12],[5],[4],[11],[12],[12],[0],[11],[15],[15],[7],[12],[12],[7],[2],[12],[0],[7],[0],[14],[3],[2],[6],[9],[11],[15],[3],[11],[7],[7],[12],[15],[11],[12],[10],[12],[5],[15],[3],[5],[4],[10],[0],[12],[3],[6],[12],[12],[13],[12],[9],[10],[12],[12],[12],[2],[12],[12],[12],[12],[12],[12],[12],[13],[0],[8],[12],[12],[15],[12],[12],[4],[12],[2],[6],[14],[12],[7],[12],[15],[8],[12],[12],[8],[0],[0],[0],[12],[15],[14],[12],[12],[14],[12],[12],[4],[11],[12],[12],[12],[4],[12],[12],[12],[12],[2],[5],[5],[12],[12],[5],[12],[3],[12],[7],[3],[12],[12],[12],[12],[12],[12],[12],[12],[0],[0],[15],[12],[3],[5],[4],[12],[5],[12],[15],[3],[2],[15],[12],[12],[13],[1],[0],[11],[13],[12],[12],[14],[9],[12],[10],[15],[12],[12],[12],[1],[15],[4],[8],[12],[12],[13],[12],[13],[12],[10],[8],[6],[3],[10],[12],[10],[7],[15],[1],[12],[5],[12],[15],[15],[12],[12],[1]]]
CAP = 392
YW = 392
def setup_inputs(rng):
    return {"x": rng.standard_normal((N, 128, T), dtype=np.float32)}
def reference(x):
    y = np.full((N, 128, YW), np.nan, x.dtype)
    fill = [0] * N
    for r in range(N):
        for t in range(T):
            for e in ROUTE[r][t]:
                if fill[e] < CAP:
                    y[e][:, fill[e]] = x[r][:, t]
                fill[e] += 1
    return {"y": y}

@@ -1,0 +1,298 @@
+from concourse.bass import DstId, RemoteDMATransfer
+
+SCRATCH = {
+    "xs": ("sbuf", [128, 512], "float32"),
+    "land": ("sbuf", [128, 392], "float32"),
+}
+SEMAPHORES = ["loaded", "got", "sent", "arrived", "stored"]
+
+GROUP = 4
+ISSUE = 32
+HOP = 64
+ROWBYTES = 512
+CALLW = 32
+
+SHARE = {0: [], 1: [8], 2: [4, 4], 3: [4, 2, 2], 4: [2, 2, 2, 2], 5: [2, 2, 2, 1, 1], 6: [2, 2, 1, 1, 1, 1],
+         7: [2, 1, 1, 1, 1, 1, 1], 8: [1, 1, 1, 1, 1, 1, 1, 1]}
+TAIL = {0: [], 1: [[8]], 2: [[4, 4]], 3: [[4, 4], [8]], 4: [[2, 2, 2, 2]], 5: [[2, 2, 2, 2], [8]],
+        6: [[2, 2, 2, 2], [4, 4]], 7: [[2, 1, 1, 1, 1, 1, 1]]}
+PLAN = {}
+
+
+def frows(n):
+    return 128 * (n // 8) + (128 if n % 8 == 7 else 16 * (n % 8))
+
+
+def capn(budget):
+    n = 0
+    while frows(n + 1) <= budget:
+        n += 1
+    return n
+
+
+def make_jobs(route, ntok, cap):
+    n = len(route)
+    fill = [0] * n
+    jobs = [[] for _ in range(n)]
+    for r in range(n):
+        for t in range(ntok):
+            e = route[r][t][0]
+            if fill[e] < cap:
+                j = jobs[r]
+                if j and j[-1][2] == e and j[-1][0] + j[-1][1] == t:
+                    j[-1][1] += 1
+                else:
+                    j.append([t, 1, e, fill[e]])
+            fill[e] += 1
+    return jobs, [min(v, cap) for v in fill]
+
+
+def capable(c):
+    return c % 8 in (2, 3, 6, 7)
+
+
+def arrivals(rc, calls, widths):
+    busy = [0.0] * 16
+    arr = {}
+    for k, (a, b) in enumerate(calls):
+        ti = (k + 1) * ISSUE
+        c1 = 1 + 4 * widths[k] / ROWBYTES
+        for lst, base in ((b, 0), (a, 8)):
+            e = base
+            for w, m in zip(lst, SHARE[len(lst)]):
+                en = max([ti] + busy[e:e + m]) + 128 / m * c1
+                for v in range(e, e + m):
+                    busy[v] = en
+                arr[w] = en + HOP
+                e += m
+    arr[rc] = max(max(busy[:8]), len(calls) * ISSUE)
+    return arr
+
+
+def plan_rank(r, cores, jobs, on, off, par):
+    rc = cores[r]
+    calls = []
+    i = 0
+    while i < len(on) or i < len(off):
+        calls.append((on[i:i + GROUP], off[i:i + GROUP]))
+        i += GROUP
+    widths = [70] * len(calls)
+    streams = [[j for j in jobs if par(cores[j[2]]) == q] for q in (0, 1)]
+    order = [w for a, b in calls for w in a + b]
+    order.insert(max(0, len(order) - 1), rc)
+    best = None
+    for it in range(6):
+        arr = arrivals(rc, calls, widths)
+
+        def greedy(tau):
+            p = [0, 0]
+            asg = {}
+            quota = {w: capn(tau - arr[w] - ISSUE) for w in order}
+            for idx, w in enumerate(order):
+                mine = []
+                n = quota[w]
+
+                def take(q, lim):
+                    c = 0
+                    while p[q] < len(streams[q]):
+                        jb = streams[q][p[q]]
+                        wt = 0 if cores[jb[2]] // 8 == w // 8 else 1
+                        if c + wt > lim or (w == rc and jb[2] == r):
+                            break
+                        c += wt
+                        mine.append(jb)
+                        p[q] += 1
+                    return c
+                if not capable(w):
+                    take(par(w), n)
+                else:
+                    d = [len(streams[q]) - p[q]
+                         - sum(quota[v] for v in order[idx + 1:] if not capable(v) and par(v) == q) for q in (0, 1)]
+                    q = 0 if d[0] >= d[1] else 1
+                    if w == rc:
+                        q = 1 - par(rc)
+                    c = take(q, min(n, max(d[q], 0)))
+                    if c < n:
+                        take(1 - q, min(n - c, max(d[1 - q], 0)))
+                asg[w] = mine
+            return p[0] == len(streams[0]) and p[1] == len(streams[1]), asg
+        lo, hi = 0, 8000
+        while hi - lo > 2:
+            mid = (lo + hi) / 2
+            if greedy(mid)[0]:
+                hi = mid
+            else:
+                lo = mid
+        asg = greedy(hi)[1]
+        nw = []
+        for a, b in calls:
+            ws = [max(j[0] + j[1] for j in asg[w]) - min(j[0] for j in asg[w]) for w in a + b if asg[w]]
+            nw.append(max(ws) if ws else 1)
+        arr2 = arrivals(rc, calls, nw)
+        real = max(arr2[w] + ISSUE + frows(sum(1 for j in asg[w] if cores[j[2]] // 8 != w // 8)) for w in order)
+        if best is None or real < best[0]:
+            best = (real, asg, calls, nw)
+        widths = [(u + v) / 2 for u, v in zip(widths, nw)]
+    return best
+
+
+def layered(w, jobs, cores, maxw):
+    pcs = []
+    for t, wd, d, p in jobs:
+        while wd > maxw:
+            s = maxw if wd - maxw != 1 or maxw == 1 else maxw - 1
+            pcs.append([t, s, d, p])
+            t += s
+            p += s
+            wd -= s
+        pcs.append([t, wd, d, p])
+    off = [j for j in pcs if cores[j[2]] // 8 != w // 8]
+    onc = [j for j in pcs if cores[j[2]] // 8 == w // 8]
+    cw = {}
+    for j in off:
+        cw[j[1]] = cw.get(j[1], 0) + 1
+    off.sort(key=lambda j: (-cw[j[1]], j[1], j[0]))
+    q, r = divmod(len(off), 8)
+    calls = []
+    i = 0
+    for sizes in [SHARE[8]] * q + TAIL[r]:
+        e = 0
+        layer = {}
+        for m in sizes:
+            layer.setdefault(off[i][1], []).append((off[i], ((1 << m) - 1) << e, m))
+            e += m
+            i += 1
+        for wd in layer:
+            calls.append([wd, layer[wd], False])
+    ow = {}
+    for j in onc:
+        ow.setdefault(j[1], []).append(j)
+    for wd in ow:
+        lst = ow[wd]
+        for s in range(0, len(lst), 8):
+            b = lst[s:s + 8]
+            e = 8
+            tr = []
+            for j, m in zip(b, SHARE[len(b)]):
+                tr.append((j, ((1 << m) - 1) << e, m))
+                e += m
+            done = False
+            for c in calls:
+                if c[0] == wd and not c[2]:
+                    c[1] = c[1] + tr
+                    c[2] = True
+                    done = True
+                    break
+            if not done:
+                calls.append([wd, tr, True])
+    calls.sort(key=lambda c: -max(128 // t[2] for t in c[1]))
+    return calls, frows(len(off))
+
+
+def pack(w, jobs, cores):
+    best = None
+    for mw in (1, 2, 3, 99):
+        c, rows = layered(w, jobs, cores, mw)
+        s = rows + CALLW * len(c)
+        if best is None or s < best[0]:
+            best = (s, c)
+    return best[1]
+
+
+def build(T, topo):
+    cores = list(T.cores)
+    ntok = T.tables["T"]
+    jobs, counts = make_jobs(T.tables["ROUTE"], ntok, T.tables["CAP"])
+    n = len(cores)
+
+    def par(c):
+        return topo.chip(c) % 2
+    heavy = sorted(range(n), key=lambda r: -len(jobs[r]))[:2]
+    on = {}
+    off = {}
+    lent = []
+    for r in range(n):
+        b = cores[r] - cores[r] % 8
+        on[r] = [b + v for v in (0, 3, 1, 6, 4, 7, 5) if b + v != cores[r]]
+        o = [0, 2, 1, 3, 4, 6, 5, 7]
+        if r not in heavy:
+            give = 5 if par(b) == 0 else 7
+            o = [v for v in o if v != give]
+            if not capable(o[-1]):
+                k = max(i for i, v in enumerate(o) if capable(v))
+                o.append(o.pop(k))
+            lent.append(b + 64 + give)
+        off[r] = [b + 64 + v for v in o]
+    lent.sort(key=capable)
+    for i, c in enumerate(lent):
+        off[heavy[i % 2]].append(c)
+    deal = {}
+    work = {}
+    arrive = [0] * n
+    for r in range(n):
+        rc = cores[r]
+        real, asg, calls, widths = plan_rank(r, cores, jobs[r], on[r], off[r], par)
+        deal[r] = []
+        for k, (a, b) in enumerate(calls):
+            wd = widths[k]
+            out = []
+            for lst, base in ((b, 0), (a, 8)):
+                lst = [w for w in lst if asg[w]]
+                e = base
+                for w, m in zip(lst, SHARE[len(lst)]):
+                    s = min(min(j[0] for j in asg[w]), ntok - wd)
+                    out.append((w, s, wd, ((1 << m) - 1) << e, m))
+                    work[w] = (s, m, pack(w, asg[w], cores))
+                    e += m
+            if out:
+                deal[r].append(out)
+        work[rc] = (0, 0, pack(rc, asg[rc], cores))
+        for w in asg:
+            if asg[w]:
+                for wd, tr, flag in work[w][2]:
+                    for j, mask, m in tr:
+                        arrive[j[2]] += m
+    return {"deal": deal, "work": work, "arrive": arrive, "counts": counts, "cores": cores}
+
+
+def rank_program(g, core, T, topo):
+    if "p" not in PLAN:
+        PLAN["p"] = build(T, topo)
+    plan = PLAN["p"]
+    cores = plan["cores"]
+    rank = T.rank_of(core)
+    if rank is None and core not in plan["work"]:
+        return
+    sent = 0
+    if rank is not None:
+        g.sync.dma_start(T.xs[:, :], T.x[:, :]).then_inc(T.sem.loaded, 16)
+        g.wait_ge(T.sem.loaded, 16)
+        for call in plan["deal"][rank]:
+            trs = []
+            for w, s, wd, mask, m in call:
+                rid, pid = topo.addr(w, core)
+                trs.append(RemoteDMATransfer(dst_ids=[DstId(rid=rid, pnc=pid)], dma_engine_mask=mask,
+                                             remote_sem=T.sem.got, src=T.xs[:, s:s + wd], dst=T.xs[:, 0:wd]))
+                sent += m
+            g.remote_dma_fused(trs, local_sem=T.sem.sent)
+    start, need, calls = plan["work"][core]
+    if rank is None:
+        g.wait_ge(T.sem.got, need)
+    for wd, tr, flag in calls:
+        trs = []
+        for j, mask, m in tr:
+            d = cores[j[2]]
+            rid, pid = topo.addr(d, core)
+            a = j[0] - start
+            trs.append(RemoteDMATransfer(dst_ids=[DstId(rid=rid, pnc=pid)], dma_engine_mask=mask,
+                                         remote_sem=T.sem.arrived, src=T.xs[:, a:a + wd],
+                                         dst=T.land[:, j[3]:j[3] + wd]))
+            sent += m
+        g.remote_dma_fused(trs, local_sem=T.sem.sent)
+    if rank is not None:
+        cnt = plan["counts"][rank]
+        g.sync.wait_ge(T.sem.arrived, plan["arrive"][rank])
+        g.sync.dma_start(T.y[:, 0:cnt], T.land[:, 0:cnt]).then_inc(T.sem.stored, 16)
+        g.sync.wait_ge(T.sem.stored, 16)
+    if sent:
+        g.wait_ge(T.sem.sent, sent)

@@ -6,28 +6,49 @@ SCRATCH = {
 }
 SEMAPHORES = ["loaded", "got", "sent", "arrived", "stored"]
 
-GROUP = 4
-ISSUE = 32
+GROUP = 8
+CHAIN = 4
+WIDTHS = (48, 56, 64, 72, 80, 96)
+ISSUE = 64
 HOP = 64
 ROWBYTES = 512
-CALLW = 32
+PORT = 1024
 
 SHARE = {0: [], 1: [8], 2: [4, 4], 3: [4, 2, 2], 4: [2, 2, 2, 2], 5: [2, 2, 2, 1, 1], 6: [2, 2, 1, 1, 1, 1],
          7: [2, 1, 1, 1, 1, 1, 1], 8: [1, 1, 1, 1, 1, 1, 1, 1]}
-TAIL = {0: [], 1: [[8]], 2: [[4, 4]], 3: [[4, 4], [8]], 4: [[2, 2, 2, 2]], 5: [[2, 2, 2, 2], [8]],
-        6: [[2, 2, 2, 2], [4, 4]], 7: [[2, 1, 1, 1, 1, 1, 1]]}
+SPLIT = {3: [[4, 4], [8]], 5: [[2, 2, 2, 2], [8]], 6: [[2, 2, 2, 2], [4, 4]]}
 PLAN = {}
 
 
-def frows(n):
-    return 128 * (n // 8) + (128 if n % 8 == 7 else 16 * (n % 8))
+def finish(layers, t0, eng0):
+    t = t0
+    eng = eng0
+    for rows in sorted([128 // min(c) for c in layers], reverse=True):
+        t += ISSUE
+        eng = max(eng, t) + rows
+    return eng
 
 
-def capn(budget):
-    n = 0
-    while frows(n + 1) <= budget:
-        n += 1
-    return n
+def shapes(n):
+    q, r = divmod(n, 8)
+    full = [SHARE[8]] * q
+    out = [full + ([SHARE[r]] if r else [])]
+    if r in SPLIT:
+        out.append(full + SPLIT[r])
+    return out
+
+
+def choose(s, d, t0, eng0, kmax):
+    best = None
+    for cut2, ns, nd in ((False, s, d), (True, s + 2 * d, 0)):
+        for a in shapes(ns):
+            for b in shapes(nd):
+                f = finish(a + b, t0, eng0) if len(a) + len(b) <= kmax else 1e9
+                if best is None or f < best[0]:
+                    best = (f, a, b, cut2)
+        if d == 0:
+            break
+    return best
 
 
 def make_jobs(route, ntok, cap):
@@ -39,7 +60,7 @@ def make_jobs(route, ntok, cap):
             e = route[r][t][0]
             if fill[e] < cap:
                 j = jobs[r]
-                if j and j[-1][2] == e and j[-1][0] + j[-1][1] == t:
+                if j and j[-1][2] == e and j[-1][0] + j[-1][1] == t and j[-1][1] < 2:
                     j[-1][1] += 1
                 else:
                     j.append([t, 1, e, fill[e]])
@@ -54,22 +75,26 @@ def capable(c):
 def arrivals(rc, calls, widths):
     busy = [0.0] * 16
     arr = {}
+    port = 0.0
     for k, (a, b) in enumerate(calls):
         ti = (k + 1) * ISSUE
         c1 = 1 + 4 * widths[k] / ROWBYTES
+        port = max(port, ti) + len(b) * 512 * widths[k] / PORT
         for lst, base in ((b, 0), (a, 8)):
             e = base
             for w, m in zip(lst, SHARE[len(lst)]):
                 en = max([ti] + busy[e:e + m]) + 128 / m * c1
+                if base == 0:
+                    en = max(en, port)
                 for v in range(e, e + m):
                     busy[v] = en
-                arr[w] = en + HOP
+                arr[w] = (en + HOP, 0.0, CHAIN - 1 - k)
                 e += m
-    arr[rc] = max(max(busy[:8]), len(calls) * ISSUE)
+    arr[rc] = (len(calls) * ISSUE, max(busy[:8]), CHAIN - len(calls))
     return arr
 
 
-def plan_rank(r, cores, jobs, on, off, par):
+def plan_rank(r, cores, jobs, on, off, par, wmax):
     rc = cores[r]
     calls = []
     i = 0
@@ -87,116 +112,113 @@ def plan_rank(r, cores, jobs, on, off, par):
         def greedy(tau):
             p = [0, 0]
             asg = {}
-            quota = {w: capn(tau - arr[w] - ISSUE) for w in order}
+            quota = {}
+            for w in order:
+                n = 0
+                while n < 64 and choose(n + 1, 0, arr[w][0], arr[w][1], arr[w][2])[0] <= tau:
+                    n += 1
+                quota[w] = n
             for idx, w in enumerate(order):
                 mine = []
-                n = quota[w]
+                cnt = [0, 0, 0]
 
                 def take(q, lim):
                     c = 0
-                    while p[q] < len(streams[q]):
+                    while p[q] < len(streams[q]) and c < lim:
                         jb = streams[q][p[q]]
-                        wt = 0 if cores[jb[2]] // 8 == w // 8 else 1
-                        if c + wt > lim or (w == rc and jb[2] == r):
+                        if w == rc and jb[2] == r:
                             break
-                        c += wt
+                        if w != rc and mine and (max(jb[0] + jb[1], max(v[0] + v[1] for v in mine))
+                                                 - min(jb[0], min(v[0] for v in mine))) > wmax:
+                            break
+                        if cores[jb[2]] // 8 != w // 8:
+                            cnt[jb[1]] += 1
+                            if choose(cnt[1], cnt[2], arr[w][0], arr[w][1], arr[w][2])[0] > tau:
+                                cnt[jb[1]] -= 1
+                                break
+                            c += 1
                         mine.append(jb)
                         p[q] += 1
                     return c
                 if not capable(w):
-                    take(par(w), n)
+                    take(par(w), 999)
                 else:
                     d = [len(streams[q]) - p[q]
                          - sum(quota[v] for v in order[idx + 1:] if not capable(v) and par(v) == q) for q in (0, 1)]
                     q = 0 if d[0] >= d[1] else 1
                     if w == rc:
                         q = 1 - par(rc)
-                    c = take(q, min(n, max(d[q], 0)))
-                    if c < n:
-                        take(1 - q, min(n - c, max(d[1 - q], 0)))
+                    take(q, max(d[q], 0))
+                    take(1 - q, max(d[1 - q], 0))
                 asg[w] = mine
             return p[0] == len(streams[0]) and p[1] == len(streams[1]), asg
-        lo, hi = 0, 8000
-        while hi - lo > 2:
+        lo, hi = 0, 16000
+        while hi - lo > 4:
             mid = (lo + hi) / 2
             if greedy(mid)[0]:
                 hi = mid
             else:
                 lo = mid
-        asg = greedy(hi)[1]
+        ok, asg = greedy(hi)
+        if not ok:
+            continue
         nw = []
         for a, b in calls:
             ws = [max(j[0] + j[1] for j in asg[w]) - min(j[0] for j in asg[w]) for w in a + b if asg[w]]
             nw.append(max(ws) if ws else 1)
         arr2 = arrivals(rc, calls, nw)
-        real = max(arr2[w] + ISSUE + frows(sum(1 for j in asg[w] if cores[j[2]] // 8 != w // 8)) for w in order)
+        real = 0
+        for w in order:
+            far = [j for j in asg[w] if cores[j[2]] // 8 != w // 8]
+            real = max(real, choose(sum(1 for j in far if j[1] == 1), sum(1 for j in far if j[1] == 2),
+                                    arr2[w][0], arr2[w][1], arr2[w][2])[0])
         if best is None or real < best[0]:
-            best = (real, asg, calls, nw)
+            best = (real, asg, calls, nw, arr2)
         widths = [(u + v) / 2 for u, v in zip(widths, nw)]
     return best
 
 
-def layered(w, jobs, cores, maxw):
-    pcs = []
-    for t, wd, d, p in jobs:
-        while wd > maxw:
-            s = maxw if wd - maxw != 1 or maxw == 1 else maxw - 1
-            pcs.append([t, s, d, p])
-            t += s
-            p += s
-            wd -= s
-        pcs.append([t, wd, d, p])
-    off = [j for j in pcs if cores[j[2]] // 8 != w // 8]
-    onc = [j for j in pcs if cores[j[2]] // 8 == w // 8]
-    cw = {}
-    for j in off:
-        cw[j[1]] = cw.get(j[1], 0) + 1
-    off.sort(key=lambda j: (-cw[j[1]], j[1], j[0]))
-    q, r = divmod(len(off), 8)
+def cut(j):
+    return [[j[0] + k, 1, j[2], j[3] + k] for k in range(j[1])]
+
+
+def pack(w, jobs, cores, t0, eng0, kmax):
+    far = [j for j in jobs if cores[j[2]] // 8 != w // 8]
+    near = [p for j in jobs if cores[j[2]] // 8 == w // 8 for p in cut(j)]
+    one = [j for j in far if j[1] == 1]
+    two = [j for j in far if j[1] == 2]
+    f, a, b, docut = choose(len(one), len(two), t0, eng0, kmax)
+    if docut:
+        one = one + [p for j in two for p in cut(j)]
+        two = []
     calls = []
-    i = 0
-    for sizes in [SHARE[8]] * q + TAIL[r]:
-        e = 0
-        layer = {}
-        for m in sizes:
-            layer.setdefault(off[i][1], []).append((off[i], ((1 << m) - 1) << e, m))
-            e += m
-            i += 1
-        for wd in layer:
-            calls.append([wd, layer[wd], False])
-    ow = {}
-    for j in onc:
-        ow.setdefault(j[1], []).append(j)
-    for wd in ow:
-        lst = ow[wd]
-        for s in range(0, len(lst), 8):
-            b = lst[s:s + 8]
-            e = 8
+    for wd, lst, lay in ((1, one, a), (2, two, b)):
+        i = 0
+        for sizes in lay:
+            e = 0
             tr = []
-            for j, m in zip(b, SHARE[len(b)]):
-                tr.append((j, ((1 << m) - 1) << e, m))
+            for m in sizes:
+                tr.append((lst[i], ((1 << m) - 1) << e, m))
                 e += m
-            done = False
-            for c in calls:
-                if c[0] == wd and not c[2]:
-                    c[1] = c[1] + tr
-                    c[2] = True
-                    done = True
-                    break
-            if not done:
-                calls.append([wd, tr, True])
+                i += 1
+            calls.append([wd, tr])
     calls.sort(key=lambda c: -max(128 // t[2] for t in c[1]))
-    return calls, frows(len(off))
-
-
-def pack(w, jobs, cores):
-    best = None
-    for mw in (1, 2, 3, 99):
-        c, rows = layered(w, jobs, cores, mw)
-        s = rows + CALLW * len(c)
-        if best is None or s < best[0]:
-            best = (s, c)
-    return best[1]
+    k = 0
+    for s in range(0, len(near), 8):
+        blk = near[s:s + 8]
+        e = 8
+        tr = []
+        for j, m in zip(blk, SHARE[len(blk)]):
+            tr.append((j, ((1 << m) - 1) << e, m))
+            e += m
+        while k < len(calls) and calls[k][0] != 1:
+            k += 1
+        if k < len(calls):
+            calls[k][1] = calls[k][1] + tr
+        else:
+            calls.append([1, tr])
+        k += 1
+    return calls
 
 
 def build(T, topo):
@@ -231,7 +253,8 @@ def build(T, topo):
     arrive = [0] * n
     for r in range(n):
         rc = cores[r]
-        real, asg, calls, widths = plan_rank(r, cores, jobs[r], on[r], off[r], par)
+        plans = [plan_rank(r, cores, jobs[r], on[r], off[r], par, wm) for wm in WIDTHS]
+        real, asg, calls, widths, arr = min([p for p in plans if p is not None], key=lambda p: p[0])
         deal[r] = []
         for k, (a, b) in enumerate(calls):
             wd = widths[k]
@@ -242,14 +265,14 @@ def build(T, topo):
                 for w, m in zip(lst, SHARE[len(lst)]):
                     s = min(min(j[0] for j in asg[w]), ntok - wd)
                     out.append((w, s, wd, ((1 << m) - 1) << e, m))
-                    work[w] = (s, m, pack(w, asg[w], cores))
+                    work[w] = (s, m, pack(w, asg[w], cores, arr[w][0], arr[w][1], arr[w][2]))
                     e += m
             if out:
                 deal[r].append(out)
-        work[rc] = (0, 0, pack(rc, asg[rc], cores))
+        work[rc] = (0, 0, pack(rc, asg[rc], cores, arr[rc][0], arr[rc][1], arr[rc][2]))
         for w in asg:
             if asg[w]:
-                for wd, tr, flag in work[w][2]:
+                for wd, tr in work[w][2]:
                     for j, mask, m in tr:
                         arrive[j[2]] += m
     return {"deal": deal, "work": work, "arrive": arrive, "counts": counts, "cores": cores}
@@ -278,7 +301,7 @@ def rank_program(g, core, T, topo):
     start, need, calls = plan["work"][core]
     if rank is None:
         g.wait_ge(T.sem.got, need)
-    for wd, tr, flag in calls:
+    for wd, tr in calls:
         trs = []
         for j, mask, m in tr:
             d = cores[j[2]]

from concourse.bass import DstId, RemoteDMATransfer

SCRATCH = {
    "xs": ("sbuf", [128, 512], "float32"),
    "land": ("sbuf", [128, 392], "float32"),
}
SEMAPHORES = ["loaded", "got", "sent", "arrived", "stored"]

GROUP = 8
CHAIN = 4
WIDTHS = (48, 56, 64, 72, 80, 96)
ISSUE = 64
HOP = 64
ROWBYTES = 512
PORT = 1024

SHARE = {0: [], 1: [8], 2: [4, 4], 3: [4, 2, 2], 4: [2, 2, 2, 2], 5: [2, 2, 2, 1, 1], 6: [2, 2, 1, 1, 1, 1],
         7: [2, 1, 1, 1, 1, 1, 1], 8: [1, 1, 1, 1, 1, 1, 1, 1]}
SPLIT = {3: [[4, 4], [8]], 5: [[2, 2, 2, 2], [8]], 6: [[2, 2, 2, 2], [4, 4]]}
PLAN = {}


def finish(layers, t0, eng0):
    t = t0
    eng = eng0
    for rows in sorted([128 // min(c) for c in layers], reverse=True):
        t += ISSUE
        eng = max(eng, t) + rows
    return eng


def shapes(n):
    q, r = divmod(n, 8)
    full = [SHARE[8]] * q
    out = [full + ([SHARE[r]] if r else [])]
    if r in SPLIT:
        out.append(full + SPLIT[r])
    return out


def choose(s, d, t0, eng0, kmax):
    best = None
    for cut2, ns, nd in ((False, s, d), (True, s + 2 * d, 0)):
        for a in shapes(ns):
            for b in shapes(nd):
                f = finish(a + b, t0, eng0) if len(a) + len(b) <= kmax else 1e9
                if best is None or f < best[0]:
                    best = (f, a, b, cut2)
        if d == 0:
            break
    return best


def make_jobs(route, ntok, cap):
    n = len(route)
    fill = [0] * n
    jobs = [[] for _ in range(n)]
    for r in range(n):
        for t in range(ntok):
            e = route[r][t][0]
            if fill[e] < cap:
                j = jobs[r]
                if j and j[-1][2] == e and j[-1][0] + j[-1][1] == t and j[-1][1] < 2:
                    j[-1][1] += 1
                else:
                    j.append([t, 1, e, fill[e]])
            fill[e] += 1
    return jobs, [min(v, cap) for v in fill]


def capable(c):
    return c % 8 in (2, 3, 6, 7)


def arrivals(rc, calls, widths):
    busy = [0.0] * 16
    arr = {}
    port = 0.0
    for k, (a, b) in enumerate(calls):
        ti = (k + 1) * ISSUE
        c1 = 1 + 4 * widths[k] / ROWBYTES
        port = max(port, ti) + len(b) * 512 * widths[k] / PORT
        for lst, base in ((b, 0), (a, 8)):
            e = base
            for w, m in zip(lst, SHARE[len(lst)]):
                en = max([ti] + busy[e:e + m]) + 128 / m * c1
                if base == 0:
                    en = max(en, port)
                for v in range(e, e + m):
                    busy[v] = en
                arr[w] = (en + HOP, 0.0, CHAIN - 1 - k)
                e += m
    arr[rc] = (len(calls) * ISSUE, max(busy[:8]), CHAIN - len(calls))
    return arr


def plan_rank(r, cores, jobs, on, off, par, wmax):
    rc = cores[r]
    calls = []
    i = 0
    while i < len(on) or i < len(off):
        calls.append((on[i:i + GROUP], off[i:i + GROUP]))
        i += GROUP
    widths = [70] * len(calls)
    streams = [[j for j in jobs if par(cores[j[2]]) == q] for q in (0, 1)]
    order = [w for a, b in calls for w in a + b]
    order.insert(max(0, len(order) - 1), rc)
    best = None
    for it in range(6):
        arr = arrivals(rc, calls, widths)

        def greedy(tau):
            p = [0, 0]
            asg = {}
            quota = {}
            for w in order:
                n = 0
                while n < 64 and choose(n + 1, 0, arr[w][0], arr[w][1], arr[w][2])[0] <= tau:
                    n += 1
                quota[w] = n
            for idx, w in enumerate(order):
                mine = []
                cnt = [0, 0, 0]

                def take(q, lim):
                    c = 0
                    while p[q] < len(streams[q]) and c < lim:
                        jb = streams[q][p[q]]
                        if w == rc and jb[2] == r:
                            break
                        if w != rc and mine and (max(jb[0] + jb[1], max(v[0] + v[1] for v in mine))
                                                 - min(jb[0], min(v[0] for v in mine))) > wmax:
                            break
                        if cores[jb[2]] // 8 != w // 8:
                            cnt[jb[1]] += 1
                            if choose(cnt[1], cnt[2], arr[w][0], arr[w][1], arr[w][2])[0] > tau:
                                cnt[jb[1]] -= 1
                                break
                            c += 1
                        mine.append(jb)
                        p[q] += 1
                    return c
                if not capable(w):
                    take(par(w), 999)
                else:
                    d = [len(streams[q]) - p[q]
                         - sum(quota[v] for v in order[idx + 1:] if not capable(v) and par(v) == q) for q in (0, 1)]
                    q = 0 if d[0] >= d[1] else 1
                    if w == rc:
                        q = 1 - par(rc)
                    take(q, max(d[q], 0))
                    take(1 - q, max(d[1 - q], 0))
                asg[w] = mine
            return p[0] == len(streams[0]) and p[1] == len(streams[1]), asg
        lo, hi = 0, 16000
        while hi - lo > 4:
            mid = (lo + hi) / 2
            if greedy(mid)[0]:
                hi = mid
            else:
                lo = mid
        ok, asg = greedy(hi)
        if not ok:
            continue
        nw = []
        for a, b in calls:
            ws = [max(j[0] + j[1] for j in asg[w]) - min(j[0] for j in asg[w]) for w in a + b if asg[w]]
            nw.append(max(ws) if ws else 1)
        arr2 = arrivals(rc, calls, nw)
        real = 0
        for w in order:
            far = [j for j in asg[w] if cores[j[2]] // 8 != w // 8]
            real = max(real, choose(sum(1 for j in far if j[1] == 1), sum(1 for j in far if j[1] == 2),
                                    arr2[w][0], arr2[w][1], arr2[w][2])[0])
        if best is None or real < best[0]:
            best = (real, asg, calls, nw, arr2)
        widths = [(u + v) / 2 for u, v in zip(widths, nw)]
    return best


def cut(j):
    return [[j[0] + k, 1, j[2], j[3] + k] for k in range(j[1])]


def pack(w, jobs, cores, t0, eng0, kmax):
    far = [j for j in jobs if cores[j[2]] // 8 != w // 8]
    near = [p for j in jobs if cores[j[2]] // 8 == w // 8 for p in cut(j)]
    one = [j for j in far if j[1] == 1]
    two = [j for j in far if j[1] == 2]
    f, a, b, docut = choose(len(one), len(two), t0, eng0, kmax)
    if docut:
        one = one + [p for j in two for p in cut(j)]
        two = []
    calls = []
    for wd, lst, lay in ((1, one, a), (2, two, b)):
        i = 0
        for sizes in lay:
            e = 0
            tr = []
            for m in sizes:
                tr.append((lst[i], ((1 << m) - 1) << e, m))
                e += m
                i += 1
            calls.append([wd, tr])
    calls.sort(key=lambda c: -max(128 // t[2] for t in c[1]))
    k = 0
    for s in range(0, len(near), 8):
        blk = near[s:s + 8]
        e = 8
        tr = []
        for j, m in zip(blk, SHARE[len(blk)]):
            tr.append((j, ((1 << m) - 1) << e, m))
            e += m
        while k < len(calls) and calls[k][0] != 1:
            k += 1
        if k < len(calls):
            calls[k][1] = calls[k][1] + tr
        else:
            calls.append([1, tr])
        k += 1
    return calls


def build(T, topo):
    cores = list(T.cores)
    ntok = T.tables["T"]
    jobs, counts = make_jobs(T.tables["ROUTE"], ntok, T.tables["CAP"])
    n = len(cores)

    def par(c):
        return topo.chip(c) % 2
    heavy = sorted(range(n), key=lambda r: -len(jobs[r]))[:2]
    on = {}
    off = {}
    lent = []
    for r in range(n):
        b = cores[r] - cores[r] % 8
        on[r] = [b + v for v in (0, 3, 1, 6, 4, 7, 5) if b + v != cores[r]]
        o = [0, 2, 1, 3, 4, 6, 5, 7]
        if r not in heavy:
            give = 5 if par(b) == 0 else 7
            o = [v for v in o if v != give]
            if not capable(o[-1]):
                k = max(i for i, v in enumerate(o) if capable(v))
                o.append(o.pop(k))
            lent.append(b + 64 + give)
        off[r] = [b + 64 + v for v in o]
    lent.sort(key=capable)
    for i, c in enumerate(lent):
        off[heavy[i % 2]].append(c)
    deal = {}
    work = {}
    arrive = [0] * n
    for r in range(n):
        rc = cores[r]
        plans = [plan_rank(r, cores, jobs[r], on[r], off[r], par, wm) for wm in WIDTHS]
        real, asg, calls, widths, arr = min([p for p in plans if p is not None], key=lambda p: p[0])
        deal[r] = []
        for k, (a, b) in enumerate(calls):
            wd = widths[k]
            out = []
            for lst, base in ((b, 0), (a, 8)):
                lst = [w for w in lst if asg[w]]
                e = base
                for w, m in zip(lst, SHARE[len(lst)]):
                    s = min(min(j[0] for j in asg[w]), ntok - wd)
                    out.append((w, s, wd, ((1 << m) - 1) << e, m))
                    work[w] = (s, m, pack(w, asg[w], cores, arr[w][0], arr[w][1], arr[w][2]))
                    e += m
            if out:
                deal[r].append(out)
        work[rc] = (0, 0, pack(rc, asg[rc], cores, arr[rc][0], arr[rc][1], arr[rc][2]))
        for w in asg:
            if asg[w]:
                for wd, tr in work[w][2]:
                    for j, mask, m in tr:
                        arrive[j[2]] += m
    return {"deal": deal, "work": work, "arrive": arrive, "counts": counts, "cores": cores}


def rank_program(g, core, T, topo):
    if "p" not in PLAN:
        PLAN["p"] = build(T, topo)
    plan = PLAN["p"]
    cores = plan["cores"]
    rank = T.rank_of(core)
    if rank is None and core not in plan["work"]:
        return
    sent = 0
    if rank is not None:
        g.sync.dma_start(T.xs[:, :], T.x[:, :]).then_inc(T.sem.loaded, 16)
        g.wait_ge(T.sem.loaded, 16)
        for call in plan["deal"][rank]:
            trs = []
            for w, s, wd, mask, m in call:
                rid, pid = topo.addr(w, core)
                trs.append(RemoteDMATransfer(dst_ids=[DstId(rid=rid, pnc=pid)], dma_engine_mask=mask,
                                             remote_sem=T.sem.got, src=T.xs[:, s:s + wd], dst=T.xs[:, 0:wd]))
                sent += m
            g.remote_dma_fused(trs, local_sem=T.sem.sent)
    start, need, calls = plan["work"][core]
    if rank is None:
        g.wait_ge(T.sem.got, need)
    for wd, tr in calls:
        trs = []
        for j, mask, m in tr:
            d = cores[j[2]]
            rid, pid = topo.addr(d, core)
            a = j[0] - start
            trs.append(RemoteDMATransfer(dst_ids=[DstId(rid=rid, pnc=pid)], dma_engine_mask=mask,
                                         remote_sem=T.sem.arrived, src=T.xs[:, a:a + wd],
                                         dst=T.land[:, j[3]:j[3] + wd]))
            sent += m
        g.remote_dma_fused(trs, local_sem=T.sem.sent)
    if rank is not None:
        cnt = plan["counts"][rank]
        g.sync.wait_ge(T.sem.arrived, plan["arrive"][rank])
        g.sync.dma_start(T.y[:, 0:cnt], T.land[:, 0:cnt]).then_inc(T.sem.stored, 16)
        g.sync.wait_ge(T.sem.stored, 16)
    if sent:
        g.wait_ge(T.sem.sent, sent)
